import numpy as np, ml_dtypes
CORES = [37,45,53,61,69,109,117,125]
N = 8
import mx_ref
NC, KT, ROOT = 512, 1, 0
BF = ml_dtypes.bfloat16
def cut(t, i, w=512):
    return t[:, w * i:w * i + w]
def pk(c, s, i=0):
    return (np.ascontiguousarray(c[:, 512 * i:512 * i + 512]), mx_ref.live(s[:, 128 * i:128 * i + 128]))
def inputs(rng, e, E):
    def f(*shape):
        v = (rng.standard_normal(shape, dtype=np.float32) * np.exp2(rng.integers(-2, 3, shape[:-1] + (1,)))).astype(BF)
        return mx_ref.spread((v.astype(np.float32) * np.exp2(rng.integers(-E, E + 1, shape[:-2] + (1, 1))).astype(np.float32)).astype(BF), rng, e)
    def packed(k):
        c = np.zeros((N, 128, k * 512), np.uint8); s = np.zeros((N, 128, k * 128), np.uint8)
        for r in range(N):
            for i in range(k):
                a, b = mx_ref.quantize(f(128, 512)); c[r][:, 512 * i:512 * i + 512] = a; s[r][:, 128 * i:128 * i + 128] = mx_ref.plane(b, rng)
        return c, s
    d = {}
    d["wc"], d["ws"] = packed(KT)
    d["x"] = f(N, 128, KT * 4 * NC)
    return d
def setup_inputs(rng):
    return inputs(rng, 0, 0)
def setup_inputs_blocks(rng):
    return inputs(rng, 4, 0)
def setup_inputs_wide(rng):
    return inputs(rng, 0, 8)
def reference(wc, ws, x):
    y = np.zeros((N, 128, NC), np.float32)
    for r in range(N):
        for t in range(KT):
            p = mx_ref.matmul(pk(wc[ROOT], ws[ROOT], t), mx_ref.quantize(cut(x[r], t, 4 * NC)))
            y[r] = p if t == 0 else y[r] + p
    return {"y": y}

from concourse.bass import DstId, RemoteDMATransfer
from concourse.mybir import dt, ActivationFunctionType

SCRATCH = {
    "cd": ("dram", [128, 128], "float8_e4m3fn_x4"),
    "sd": ("dram", [128, 128], "uint8"),
    "wq": ("sbuf", [128, 128], "float8_e4m3fn_x4"),
    "wp": ("sbuf", [128, 128], "uint8"),
    "xb": ("sbuf", [128, 2048], "bfloat16"),
    "xq": ("sbuf", [128, 512], "float8_e4m3fn_x4"),
    "xp": ("sbuf", [128, 512], "uint8"),
    "ps": ("psum", [128, 1024], "float32"),
    "yb": ("sbuf", [128, 512], "float32"),
}
SEMAPHORES = ["sld", "cld", "sarr", "carr", "sent", "warr", "xld", "xqd", "mm0", "mm1", "cp", "stored"]


def _bits(mask):
    return [i for i in range(mask.bit_length()) if (mask >> i) & 1]


def _some(mask, k):
    e = _bits(mask)
    return sum(1 << i for i in e[::len(e) // k][:k])


def _plan(T, topo):
    root = T.cores[T.root]
    home = topo.chip(root)
    pool = [c for c in range(topo.CHIPS * topo.CORES_PER_CHIP)
            if topo.chip(c) == home and c != root and T.rank_of(c) is None]

    def links(d):
        ch = topo.chip(d)
        return 1 if (topo.mates(home, ch) or topo.same_plane(home, ch)) else 2

    dests = [d for d in T.cores if d != root]
    dests.sort(key=lambda d: (topo.may_write(root, d), -links(d)))
    load = {}
    plan = []
    for d in dests:
        kind = topo.may_write(root, d)
        able = [c for c in pool if topo.may_write(c, d)]
        able.sort(key=lambda c: (sum(topo.may_write(c, o) for o in dests), load.get((kind, topo.die(c)), 0),
                                 topo.die(c) != topo.die(root), c))
        f = able[0]
        pool.remove(f)
        load[(kind, topo.die(f))] = load.get((kind, topo.die(f)), 0) + 1
        plan.append((f, d))
    return plan


def rank_program(g, core, T, topo):
    S = T.sem
    u8 = dt.uint8
    root = T.cores[T.root]
    plan = _plan(T, topo)
    feeders = [f for f, _ in plan]

    inside = topo.mask(root, feeders[0])
    for f in feeders:
        inside &= topo.mask(root, f)
    m_plane = _some(inside, len(_bits(inside)) // 2)
    m_codes = inside
    n_plane, n_codes = len(_bits(m_plane)), len(_bits(m_codes))

    for f, d in plan:
        if core != f:
            continue
        rid, pid, _ = topo.addr(d)
        m = topo.mask(f, d)
        g.wait_ge(S.sarr, n_plane)
        g.remote_dma(out_ap=T.wp[:], in_ap=T.sd[:], remote_sem=S.warr, local_sem=S.sent,
                     pid=pid, routing_id=rid, dma_engine_mask=m)
        g.wait_ge(S.carr, n_codes)
        g.remote_dma(out_ap=T.wq[:].bitcast(u8), in_ap=T.cd[:].bitcast(u8), remote_sem=S.warr, local_sem=S.sent,
                     pid=pid, routing_id=rid, dma_engine_mask=m)
        g.wait_ge(S.sent, 2 * len(_bits(m)))
        return

    if T.rank_of(core) is None:
        return

    if core == root:
        g.scalar.dma_start(T.sd[:], T.ws[:]).then_inc(S.sld, 16)
        g.sync.dma_start(T.cd[:].bitcast(u8), T.wc[:]).then_inc(S.cld, 16)
        g.scalar.dma_start(T.wq[:].bitcast(u8), T.wc[:]).then_inc(S.warr, 16)
        g.scalar.dma_start(T.wp[:], T.ws[:]).then_inc(S.warr, 16)
        w_here = 32
    else:
        f = [f for f, d in plan if d == core][0]
        w_here = 2 * len(_bits(topo.mask(f, core)))
    g.sync.dma_start(T.xb[:], T.x[:]).then_inc(S.xld, 16)

    if core == root:
        ids = [DstId(rid=topo.addr(f)[0], pnc=topo.addr(f)[1]) for f in feeders]
        g.wait_ge(S.sld, 16)
        g.remote_dma_fused([RemoteDMATransfer(dst_ids=ids, dma_engine_mask=m_plane, remote_sem=S.sarr,
                                              srcs=[T.sd[:]], dsts=[T.sd[:] for _ in feeders])],
                           local_sem=S.sent)
        g.wait_ge(S.cld, 16)
        g.remote_dma_fused([RemoteDMATransfer(dst_ids=ids, dma_engine_mask=m_codes, remote_sem=S.carr,
                                              srcs=[T.cd[:].bitcast(u8)],
                                              dsts=[T.cd[:].bitcast(u8) for _ in feeders])],
                           local_sem=S.sent)

    g.vector.wait_ge(S.xld, 16)
    g.vector.quantize_mx(T.xq[:], T.xp[:], T.xb[:]).then_inc(S.xqd, 1)

    g.tensor.wait_ge(S.xqd, 1)
    g.tensor.wait_ge(S.warr, w_here)
    g.tensor.matmul_mx(T.ps[:, 0:256], T.wq[:], T.wp[:], T.xq[:, 0:256], T.xp[:, 0:256], True, True).then_inc(S.mm0, 1)
    g.tensor.matmul_mx(T.ps[:, 512:768], T.wq[:], T.wp[:], T.xq[:, 256:512], T.xp[:, 256:512], True, True).then_inc(S.mm1, 1)

    g.vector.wait_ge(S.mm0, 1)
    g.vector.tensor_copy(T.yb[:, 0:256], T.ps[:, 0:256]).then_inc(S.cp, 1)
    g.scalar.wait_ge(S.mm1, 1)
    g.scalar.activation(T.yb[:, 256:512], T.ps[:, 512:768], ActivationFunctionType.Copy).then_inc(S.cp, 1)

    if core == root:
        g.sync.wait_ge(S.sent, n_plane + n_codes)
    g.sync.wait_ge(S.cp, 2)
    g.sync.dma_start(T.y[:], T.yb[:]).then_inc(S.stored, 16)
    g.sync.wait_ge(S.stored, 16)
